import numpy as np
import ml_dtypes


def mxq(x, axis, fmt="e4m3"):
    dtype, down = {"e4m3": (ml_dtypes.float8_e4m3fn, 7), "e5m2": (ml_dtypes.float8_e5m2, 14)}[fmt]
    v = np.moveaxis(np.asarray(x, np.float32).astype(ml_dtypes.bfloat16).astype(np.float64), axis, -1)
    blocks = v.reshape(v.shape[:-1] + (-1, 32))
    amax = np.abs(blocks).max(-1, keepdims=True)
    byte = np.maximum(np.where(amax > 0, np.frexp(amax)[1] - 1 + 127, 0) - down, 1)
    scale = np.exp2(byte - 127.0)
    codes = (blocks / scale).astype(np.float32).astype(dtype).astype(np.float64)
    return np.moveaxis((codes * scale).reshape(v.shape), -1, axis)


WIDE = False


def mx_kscale(k):
    if not WIDE:
        return np.ones(k)
    levels = np.array([10, -10, 5, -5, 0])
    if k % 512:
        return np.exp2(np.random.permutation(np.resize(levels, k // 32))).repeat(32)
    a = np.empty((k // 512, 16))
    for p in range(k // 512):
        a[p, :8] = np.random.permutation(np.resize(levels, 8))
        for g in range(8):
            far = levels[np.abs(levels - a[p, g]) >= 10]
            a[p, g + 8] = far[np.random.randint(len(far))]
    return np.exp2(a.ravel()).repeat(32)


def f64(x):
    return np.asarray(x).astype(np.float64)


def striped(idx):
    return np.tile(idx.reshape(-1, 16).T, (8, 1)).astype(np.uint16)


def unstriped(offs):
    return offs[:16].T.reshape(-1).astype(np.int64)


def striped8(idx):
    return np.concatenate([x.reshape(-1, 16).T for x in idx]).astype(np.uint16)


def runs(offs, k):
    lists = np.stack([offs[16 * r : 16 * r + 16].T.reshape(-1) for r in range(8)]).astype(np.int64)
    return lists[np.arange(k) % 512 // 64]


def pack_weight(w):
    k, n = w.shape
    w = f64(np.asarray(w, np.float32).astype(ml_dtypes.bfloat16)).reshape(k // 32, 32, n)
    amax = np.abs(w).max(1)
    byte = np.clip(np.where(amax > 0, np.frexp(amax)[1] - 1 + 127 - 7, 1), 1, 254)
    scaled = (w * np.exp2(127.0 - byte)[:, None, :]).reshape(k, n).astype(np.float32)
    words = np.ascontiguousarray(scaled.reshape(k // 512, 128, 4, n).transpose(0, 1, 3, 2)).astype(ml_dtypes.float8_e4m3fn).view(np.uint8)
    return words, np.ascontiguousarray(byte.astype(np.uint8).reshape(k // 512, 16, n))


def unpack_weight(words, scales):
    g, p, n, _ = words.shape
    vals = np.ascontiguousarray(words).view(ml_dtypes.float8_e4m3fn).astype(np.float64) * np.repeat(np.exp2(scales.astype(np.float64) - 127.0), 8, axis=1)[..., None]
    return vals.transpose(0, 1, 3, 2).reshape(g * 512, n)

def planes(y):
    n, m = y.shape
    v = y.astype(np.float32).astype(ml_dtypes.bfloat16).astype(np.float64).reshape(n // 32, 32, m)
    top = np.abs(v).max(1)
    byte = np.clip(np.where(top > 0, np.frexp(top)[1] - 1 + 127 - 7, 1), 1, 254)
    codes = (v * np.exp2(127.0 - byte)[:, None, :]).reshape(n, m).astype(np.float32).astype(ml_dtypes.float8_e4m3fn).view(np.uint8)
    words = codes.reshape(n // 512, 128, 4, m).transpose(0, 1, 3, 2)
    return np.ascontiguousarray(words), np.ascontiguousarray(byte.astype(np.uint8).reshape(n // 512, 16, m))


K, T, S, N, H, G, W = 512, 2048, 512, 512, 512, 2048, 384


def setup_inputs():
    n = np.random.standard_normal
    s = mx_kscale(K)[:, None]
    u = mx_kscale(S)
    packed_xT = pack_weight(n((K, T)) * s)
    packed_w1 = pack_weight(n((K, H)) / np.sqrt(K) / s)
    packed_dT = pack_weight(n((K, G)) / s)
    packed_w2 = pack_weight(n((H, N)) / np.sqrt(H) / u[:, None])
    return {
        "x_words": packed_xT[0],
        "x_scales": packed_xT[1],
        "w1_words": packed_w1[0],
        "w1_scales": packed_w1[1],
        "d_words": packed_dT[0],
        "d_scales": packed_dT[1],
        "gn": (np.random.uniform(0.5, 1.5, (H, 1)) * u[:, None]).astype(np.float32),
        "w2_words": packed_w2[0],
        "w2_scales": packed_w2[1],
        "offs": striped(np.random.permutation(T)[:S]),
        "k1": striped8(np.random.randint(0, G, (8, H))),
        "two": striped(np.random.permutation(T)[:S]),
        "n1": striped8(np.stack([np.random.permutation(S) for _ in range(8)])),
        "n2": striped8(np.stack([np.random.permutation(S) for _ in range(8)])),
        "n3": striped8(np.stack([np.random.permutation(S) for _ in range(8)])),
        "n4": striped(np.random.permutation(S)[:W]),
        "n5": striped(np.random.permutation(S)[:W]),
    }


def reference(x_words, x_scales, w1_words, w1_scales, d_words, d_scales, gn, w2_words, w2_scales, offs, k1, two, n1, n2, n3, n4, n5):
    d_k1 = unpack_weight(d_words, d_scales)[np.arange(K)[:, None], runs(k1, K)]
    x_two = unpack_weight(x_words, x_scales)[:, unstriped(two)]
    d = 0.0625 * (d_k1.T @ x_two)
    xq = unpack_weight(x_words, x_scales)[:, unstriped(offs)]
    y = unpack_weight(w1_words, w1_scales).T @ xq
    z = f64(gn) * (d * (y[np.arange(H)[:, None], runs(n1, H)] - y) + 0.5 * ((d[np.arange(H)[:, None], runs(n3, H)]) * (y[np.arange(H)[:, None], runs(n2, H)] - y)))
    h = unpack_weight(w2_words, w2_scales).T @ mxq(z, 0, "e4m3")
    pa = h[:, unstriped(n5)]
    old = h[:, unstriped(n4)]
    ra = np.maximum(pa, 0.5 * old)
    out = h.copy()
    out[:, unstriped(n4)] = ra
    return (out,) + planes(out)

@@ -1,0 +1,240 @@
+from contextlib import ExitStack
+
+import concourse.mybir as mybir
+
+K, T, S, N, H, G, W = 512, 2048, 512, 512, 512, 2048, 384
+FLOPS = 2 * K * H * S * 2 + 2 * H * N * S
+
+F32 = mybir.dt.float32
+BF16 = mybir.dt.bfloat16
+I32 = mybir.dt.int32
+U32 = mybir.dt.uint32
+U16 = mybir.dt.uint16
+U8 = mybir.dt.uint8
+FP8X4 = mybir.dt.float8_e4m3fn_x4
+MULT = mybir.AluOpType.mult
+ADD = mybir.AluOpType.add
+SUB = mybir.AluOpType.subtract
+MAX = mybir.AluOpType.max
+COPY = mybir.ActivationFunctionType.Copy
+
+P = 128
+PACK = 4
+CHUNKS = [[0,256],[256,128],[384,128]]
+DCOPY_ON_SCALAR = []
+D3_ON_VECTOR = []
+SUBS_ON_GPSIMD = []
+
+
+def tile_picked_twkeyflowbkmax_none_po_kernel(tc, x_words, x_scales, w1_words, w1_scales, d_words, d_scales, gn, w2_words, w2_scales, offs, k1, two, n1, n2, n3, n4, n5, out_0, out_1, out_2):
+    nc = tc.nc
+    with ExitStack() as ctx:
+        pool = ctx.enter_context(tc.tile_pool(name="pool", bufs=1))
+        psum = ctx.enter_context(tc.psum_pool(name="psum", bufs=1))
+
+        def sb(name, shape, dtype):
+            return pool.tile(shape, dtype, name=name, align_bytes=64)
+
+        def load_list(name, src):
+            t = sb(name, list(src.shape), U16)
+            nc.sync.dma_start(t[:], src)
+            return t
+
+        def words_of(src):
+            return src[0].rearrange("p n r -> p (n r)").bitcast(I32)
+
+        def load_plane(eng, dst, src):
+            for q in range(4):
+                eng.dma_start(dst[32 * q : 32 * q + 4, :].bitcast(I32), src[0][4 * q : 4 * q + 4, :].bitcast(I32))
+
+        def deal(eng, dst, src):
+            eng.tensor_copy(dst[:].rearrange("p (t m) -> p m t", t=PACK), src[:].rearrange("p (m t) -> p m t", t=PACK))
+
+        def deal_words(eng, dst, src):
+            eng.tensor_copy(dst[:].rearrange("p (t m) -> p t m", t=PACK), src[:].rearrange("p (m t) -> p t m", t=PACK))
+
+        xs = sb("xs", [P, T], U8)
+        w1s = sb("w1s", [P, H], U8)
+        ds = sb("ds", [P, G], U8)
+        nc.gpsimd.memset(xs[:].bitcast(I32), 0)
+        nc.vector.memset(w1s[:].bitcast(I32), 0)
+        nc.vector.memset(ds[:].bitcast(I32), 0)
+
+        xw = sb("xw", [P, T], I32)
+        dw = sb("dw", [P, G], I32)
+        w1w = sb("w1w", [P, H], I32)
+        gn_sb = sb("gn_sb", [P, PACK], F32)
+        nc.sync.dma_start(w1w[:], words_of(w1_words))
+        load_plane(nc.sync, xs, x_scales)
+        offs_sb = load_list("offs_sb", offs)
+        nc.sync.dma_start(gn_sb[:], gn.rearrange("(p t) o -> p (t o)", t=PACK))
+        nc.sync.dma_start(xw[:], words_of(x_words))
+        load_plane(nc.sync, w1s, w1_scales)
+        two_sb = load_list("two_sb", two)
+        k1_sb = load_list("k1_sb", k1)
+        nc.sync.dma_start(ds[0:P:8, :].bitcast(I32), d_scales[0].bitcast(I32))
+        n1_sb = load_list("n1_sb", n1)
+        n2_sb = load_list("n2_sb", n2)
+        n3_sb = load_list("n3_sb", n3)
+        n4_sb = load_list("n4_sb", n4)
+        n5_sb = load_list("n5_sb", n5)
+        nc.sync.dma_start(dw[:], words_of(d_words))
+
+        gn32 = sb("gn32", [P, PACK], F32)
+        nc.scalar.activation(gn32[:], gn_sb[:], COPY, scale=0.03125)
+
+        xs_offs = sb("xs_offs", [P, S], U8)
+        xw_offs = sb("xw_offs", [P, S], I32)
+        xs_two = sb("xs_two", [P, S], U8)
+        xw_two = sb("xw_two", [P, S], I32)
+        ds_k1 = sb("ds_k1", [P, H], U8)
+        dw_k1 = sb("dw_k1", [P, H], I32)
+        w1s_d = sb("w1s_d", [P, H], U8)
+        w1w_d = sb("w1w_d", [P, H], I32)
+        w2s_d = sb("w2s_d", [P, N], U8)
+        w2w_d = sb("w2w_d", [P, N], I32)
+        ds_d = sb("ds_d", [P, H], U8)
+        dw_d = sb("dw_d", [P, H], I32)
+
+        nc.vector.tensor_copy(xs_offs[:], xs[:].indirect(offs_sb[:]))
+        deal_words(nc.vector, w1w_d, w1w)
+        nc.vector.tensor_copy(xw_offs[:].bitcast(U32), xw[:].bitcast(U32).indirect(offs_sb[:]))
+        deal(nc.vector, w1s_d, w1s)
+
+        def mx(out, w, ws, t, x, xsc):
+            cols = slice(P * t, P * (t + 1))
+            nc.tensor.matmul_mx(out, w[:, cols].bitcast(FP8X4), ws[:, cols], x.bitcast(FP8X4), xsc, start=True, stop=True)
+
+        y_ps = [psum.tile([P, S], F32, name="y_ps%d" % t, tag="bank%d" % t) for t in range(PACK)]
+        for t in range(PACK):
+            mx(y_ps[t][:], w1w_d, w1s_d, t, xw_offs[:], xs_offs[:])
+
+        nc.vector.tensor_copy(ds_k1[:], ds[:].indirect(k1_sb[:]))
+        nc.vector.tensor_copy(xw_two[:].bitcast(U32), xw[:].bitcast(U32).indirect(two_sb[:]))
+        deal(nc.vector, ds_d, ds_k1)
+        ds_p = ds_d
+        for j in range(1, 4):
+            nc.sync.dma_start(ds_p[j:P:32, :].bitcast(I32), ds_d[8 * j : P : 32, :].bitcast(I32))
+        nc.vector.tensor_copy(xs_two[:], xs[:].indirect(two_sb[:]))
+        nc.vector.tensor_copy(dw_k1[:].bitcast(U32), dw[:].bitcast(U32).indirect(k1_sb[:]))
+        deal_words(nc.vector, dw_d, dw_k1)
+        w2s = pool.tile([P, N], U8, name="w2s", tag="ds_k1", align_bytes=64)
+        nc.gpsimd.memset(w2s[:].bitcast(I32), 0)
+        load_plane(nc.sync, w2s, w2_scales)
+        w2w = pool.tile([P, N], I32, name="w2w", tag="xs", align_bytes=64)
+        nc.sync.dma_start(w2w[:], words_of(w2_words))
+        deal_words(nc.gpsimd, w2w_d, w2w)
+        deal(nc.gpsimd, w2s_d, w2s)
+
+        d_ps = [psum.tile([P, S], F32, name="d_ps%d" % t, tag="bank%d" % (PACK + t)) for t in range(PACK)]
+        for t in range(PACK):
+            mx(d_ps[t][:], dw_d, ds_p, t, xw_two[:], xs_two[:])
+
+        y = [sb("y%d" % t, [P, S], F32) for t in range(PACK)]
+        dh = [sb("dh%d" % t, [P, S], F32) for t in range(PACK)]
+        h = [sb("h%d" % t, [P, S], F32) for t in range(PACK)]
+        ab = pool.tile([P, 2 * PACK, S], F32, name="ab", tag="dw", align_bytes=64)
+        h_ps = []
+        e = [sb("e%d" % ci, [P, PACK, w], F32) for ci, (c0, w) in enumerate(CHUNKS)]
+        c = [sb("c%d" % ci, [P, PACK, w], F32) for ci, (c0, w) in enumerate(CHUNKS)]
+        z = [sb("z%d" % ci, [P, PACK * w], BF16) for ci, (c0, w) in enumerate(CHUNKS)]
+
+        def span(ci):
+            c0, w = CHUNKS[ci]
+            return w, slice(c0, c0 + w), slice(c0 // 16, (c0 + w) // 16)
+
+        def differences(ci, t):
+            w, cols, lcols = span(ci)
+            y1 = pool.tile([P, w], F32, name="y1_%d_%d" % (ci, t), tag="y1_%d" % t, align_bytes=64)
+            y2 = pool.tile([P, w], F32, name="y2_%d_%d" % (ci, t), tag="y2_%d" % t, align_bytes=64)
+            nc.scalar.activation(y1[:], y[t][:].indirect(n1_sb[:, lcols]), COPY)
+            nc.scalar.activation(y2[:], y[t][:].indirect(n2_sb[:, lcols]), COPY)
+            eng = nc.gpsimd if [ci, t] in SUBS_ON_GPSIMD else nc.vector
+            eng.tensor_tensor(ab[:, 2 * t, cols], y1[:], y[t][:, cols], SUB)
+            eng.tensor_tensor(ab[:, 2 * t + 1, cols], y2[:], y[t][:, cols], SUB)
+
+        def first_term(ci, t):
+            w, cols, lcols = span(ci)
+            nc.vector.scalar_tensor_tensor(e[ci][:, t, :], ab[:, 2 * t, cols], 2.0, dh[t][:, cols], MULT, MULT)
+
+        def second_term(ci, t):
+            w, cols, lcols = span(ci)
+            if [ci, t] in D3_ON_VECTOR:
+                nc.vector.tensor_tensor(c[ci][:, t, :], dh[t][:].indirect(n3_sb[:, lcols]), ab[:, 2 * t + 1, cols], MULT)
+            else:
+                d3 = sb("d3_%d_%d" % (ci, t), [P, w], F32)
+                nc.scalar.activation(d3[:], dh[t][:].indirect(n3_sb[:, lcols]), COPY)
+                nc.vector.tensor_tensor(c[ci][:, t, :], d3[:], ab[:, 2 * t + 1, cols], MULT)
+
+        def sum_terms(ci):
+            nc.vector.tensor_tensor(
+                z[ci][:].rearrange("p (g i t) -> p g t i", i=4, t=PACK),
+                e[ci][:].rearrange("p t (g i) -> p g t i", i=4),
+                c[ci][:].rearrange("p t (g i) -> p g t i", i=4),
+                ADD,
+            )
+
+        def last_product(ci):
+            w, cols, lcols = span(ci)
+            zw = sb("zw%d" % ci, [P, w], I32)
+            zs = sb("zs%d" % ci, [P, w], U8)
+            nc.vector.quantize_mx(zw[:].bitcast(FP8X4), zs[:], z[ci][:])
+            for t in range(PACK):
+                mx(h_ps[t][:, cols], w2w_d, w2s_d, t, zw[:], zs[:])
+
+        for t in range(PACK):
+            if t in DCOPY_ON_SCALAR:
+                nc.scalar.activation(dh[t][:], d_ps[t][:], COPY, scale=gn32[:, t : t + 1])
+            else:
+                nc.vector.tensor_scalar(dh[t][:], d_ps[t][:], gn32[:, t : t + 1], None, MULT)
+        for t in range(PACK):
+            nc.scalar.copy(y[t][:], y_ps[t][:])
+            differences(0, t)
+            first_term(0, t)
+        for t in range(PACK):
+            second_term(0, t)
+            h_ps.append(psum.tile([P, S], F32, name="h_ps%d" % t, tag="bank%d" % t))
+        for ci in range(1, len(CHUNKS)):
+            sum_terms(ci - 1)
+            for t in range(PACK):
+                differences(ci, t)
+                if t == 0:
+                    last_product(ci - 1)
+                first_term(ci, t)
+                second_term(ci, t)
+        last = len(CHUNKS) - 1
+        sum_terms(last)
+        early = slice(0, CHUNKS[last][0])
+        nc.scalar.copy(h[0][:, early], h_ps[0][:, early])
+        last_product(last)
+        nc.scalar.copy(h[0][:, span(last)[1]], h_ps[0][:, span(last)[1]])
+
+        ob = sb("ob", [P, S, PACK], BF16)
+        out_rows = out_0.rearrange("(p t) n -> t p n", t=PACK)
+        old = [sb("old%d" % t, [P, W], F32) for t in range(PACK)]
+        pa = [sb("pa%d" % t, [P, W], F32) for t in range(PACK)]
+        ra = [sb("ra%d" % t, [P, W], F32) for t in range(PACK)]
+        def look_up(t):
+            if t > 0:
+                nc.vector.tensor_copy(h[t][:], h_ps[t][:])
+            nc.scalar.activation(old[t][:], h[t][:].indirect(n4_sb[:]), COPY)
+            nc.vector.tensor_copy(pa[t][:], h[t][:].indirect(n5_sb[:]))
+            nc.vector.scalar_tensor_tensor(ra[t][:], old[t][:], 0.5, pa[t][:], MULT, MAX)
+
+        def put_back(t):
+            nc.scalar.activation(h[t][:].indirect(n4_sb[:]), ra[t][:], COPY)
+            nc.sync.dma_start(out_rows[t], h[t][:])
+            nc.vector.tensor_copy(ob[:, :, t], h[t][:])
+
+        look_up(0)
+        for t in range(PACK):
+            if t + 1 < PACK:
+                look_up(t + 1)
+            put_back(t)
+        ow = sb("ow", [P, S], I32)
+        osc = sb("osc", [P, S], U8)
+        nc.vector.quantize_mx(ow[:].bitcast(FP8X4), osc[:], ob[:].rearrange("p n t -> p (n t)"))
+        nc.sync.dma_start(words_of(out_1), ow[:])
+        for q in range(4):
+            eng = nc.scalar if q % 2 == 0 else nc.sync
+            eng.dma_start(out_2[0][4 * q : 4 * q + 4, :].bitcast(I32), osc[32 * q : 32 * q + 4, :].bitcast(I32))

@@ -21,7 +21,8 @@ COPY = mybir.ActivationFunctionType.Copy
 P = 128
 PACK = 4
 CHUNKS = [[0,256],[256,128],[384,128]]
-DCOPY_ON_SCALAR = []
+HALVES = [[0, 256], [256, 256]]
+DCOPY_ON_SCALAR = [3]
 D3_ON_VECTOR = []
 SUBS_ON_GPSIMD = []
 
@@ -43,9 +44,14 @@ def tile_picked_twkeyflowbkmax_none_po_kernel(tc, x_words, x_scales, w1_words, w
         def words_of(src):
             return src[0].rearrange("p n r -> p (n r)").bitcast(I32)
 
-        def load_plane(eng, dst, src):
+        def load_plane(eng, dst, src, k=0):
             for q in range(4):
-                eng.dma_start(dst[32 * q : 32 * q + 4, :].bitcast(I32), src[0][4 * q : 4 * q + 4, :].bitcast(I32))
+                eng.dma_start(dst[32 * q + k : 32 * q + k + 4, :].bitcast(I32), src[0][4 * q : 4 * q + 4, :].bitcast(I32))
+
+        def load_plane_everywhere(dst, src):
+            for q in range(4):
+                rows = src[0][4 * q : 4 * q + 4, :].bitcast(I32)
+                nc.sync.dma_start(dst[32 * q : 32 * q + 32, :].bitcast(I32), rows.unsqueeze(0).to_broadcast([8, 4, rows.shape[1]]))
 
         def deal(eng, dst, src):
             eng.tensor_copy(dst[:].rearrange("p (t m) -> p m t", t=PACK), src[:].rearrange("p (m t) -> p m t", t=PACK))
@@ -56,29 +62,27 @@ def tile_picked_twkeyflowbkmax_none_po_kernel(tc, x_words, x_scales, w1_words, w
         xs = sb("xs", [P, T], U8)
         w1s = sb("w1s", [P, H], U8)
         ds = sb("ds", [P, G], U8)
-        nc.gpsimd.memset(xs[:].bitcast(I32), 0)
-        nc.vector.memset(w1s[:].bitcast(I32), 0)
         nc.vector.memset(ds[:].bitcast(I32), 0)
 
         xw = sb("xw", [P, T], I32)
         dw = sb("dw", [P, G], I32)
         w1w = sb("w1w", [P, H], I32)
         gn_sb = sb("gn_sb", [P, PACK], F32)
-        nc.sync.dma_start(w1w[:], words_of(w1_words))
-        load_plane(nc.sync, xs, x_scales)
+        load_plane_everywhere(xs, x_scales)
         offs_sb = load_list("offs_sb", offs)
-        nc.sync.dma_start(gn_sb[:], gn.rearrange("(p t) o -> p (t o)", t=PACK))
-        nc.sync.dma_start(xw[:], words_of(x_words))
-        load_plane(nc.sync, w1s, w1_scales)
-        two_sb = load_list("two_sb", two)
         k1_sb = load_list("k1_sb", k1)
         nc.sync.dma_start(ds[0:P:8, :].bitcast(I32), d_scales[0].bitcast(I32))
+        nc.sync.dma_start(xw[:], words_of(x_words))
+        nc.sync.dma_start(w1w[:], words_of(w1_words))
+        load_plane_everywhere(w1s, w1_scales)
         n1_sb = load_list("n1_sb", n1)
         n2_sb = load_list("n2_sb", n2)
+        two_sb = load_list("two_sb", two)
+        nc.sync.dma_start(dw[:], words_of(d_words))
+        nc.sync.dma_start(gn_sb[:], gn.rearrange("(p t) o -> p (t o)", t=PACK))
         n3_sb = load_list("n3_sb", n3)
         n4_sb = load_list("n4_sb", n4)
         n5_sb = load_list("n5_sb", n5)
-        nc.sync.dma_start(dw[:], words_of(d_words))
 
         gn32 = sb("gn32", [P, PACK], F32)
         nc.scalar.activation(gn32[:], gn_sb[:], COPY, scale=0.03125)
@@ -97,9 +101,14 @@ def tile_picked_twkeyflowbkmax_none_po_kernel(tc, x_words, x_scales, w1_words, w
         dw_d = sb("dw_d", [P, H], I32)
 
         nc.vector.tensor_copy(xs_offs[:], xs[:].indirect(offs_sb[:]))
-        deal_words(nc.vector, w1w_d, w1w)
+        nc.vector.tensor_copy(ds_k1[:], ds[:].indirect(k1_sb[:]))
+        deal_words(nc.vector, ds_d, ds_k1)
         nc.vector.tensor_copy(xw_offs[:].bitcast(U32), xw[:].bitcast(U32).indirect(offs_sb[:]))
-        deal(nc.vector, w1s_d, w1s)
+        deal(nc.vector, w1w_d, w1w)
+        deal_words(nc.vector, w1s_d, w1s)
+        ds_p = ds_d
+        for j in range(1, 4):
+            nc.sync.dma_start(ds_p[j:P:32, :].bitcast(I32), ds_d[8 * j : P : 32, :].bitcast(I32))
 
         def mx(out, w, ws, t, x, xsc):
             cols = slice(P * t, P * (t + 1))
@@ -109,22 +118,14 @@ def tile_picked_twkeyflowbkmax_none_po_kernel(tc, x_words, x_scales, w1_words, w
         for t in range(PACK):
             mx(y_ps[t][:], w1w_d, w1s_d, t, xw_offs[:], xs_offs[:])
 
-        nc.vector.tensor_copy(ds_k1[:], ds[:].indirect(k1_sb[:]))
-        nc.vector.tensor_copy(xw_two[:].bitcast(U32), xw[:].bitcast(U32).indirect(two_sb[:]))
-        deal(nc.vector, ds_d, ds_k1)
-        ds_p = ds_d
-        for j in range(1, 4):
-            nc.sync.dma_start(ds_p[j:P:32, :].bitcast(I32), ds_d[8 * j : P : 32, :].bitcast(I32))
         nc.vector.tensor_copy(xs_two[:], xs[:].indirect(two_sb[:]))
+        nc.vector.tensor_copy(xw_two[:].bitcast(U32), xw[:].bitcast(U32).indirect(two_sb[:]))
         nc.vector.tensor_copy(dw_k1[:].bitcast(U32), dw[:].bitcast(U32).indirect(k1_sb[:]))
-        deal_words(nc.vector, dw_d, dw_k1)
-        w2s = pool.tile([P, N], U8, name="w2s", tag="ds_k1", align_bytes=64)
-        nc.gpsimd.memset(w2s[:].bitcast(I32), 0)
-        load_plane(nc.sync, w2s, w2_scales)
-        w2w = pool.tile([P, N], I32, name="w2w", tag="xs", align_bytes=64)
+        deal(nc.vector, dw_d, dw_k1)
+        w2w = pool.tile([P, N], I32, name="w2w", tag="ds_k1", align_bytes=64)
         nc.sync.dma_start(w2w[:], words_of(w2_words))
-        deal_words(nc.gpsimd, w2w_d, w2w)
-        deal(nc.gpsimd, w2s_d, w2s)
+        w2s = pool.tile([P, N], U8, name="w2s", tag="dw_k1", align_bytes=64)
+        load_plane_everywhere(w2s, w2_scales)
 
         d_ps = [psum.tile([P, S], F32, name="d_ps%d" % t, tag="bank%d" % (PACK + t)) for t in range(PACK)]
         for t in range(PACK):
@@ -135,7 +136,8 @@ def tile_picked_twkeyflowbkmax_none_po_kernel(tc, x_words, x_scales, w1_words, w
         h = [sb("h%d" % t, [P, S], F32) for t in range(PACK)]
         ab = pool.tile([P, 2 * PACK, S], F32, name="ab", tag="dw", align_bytes=64)
         h_ps = []
-        e = [sb("e%d" % ci, [P, PACK, w], F32) for ci, (c0, w) in enumerate(CHUNKS)]
+        d3 = [None] * PACK
+        e = sb("e", [P, PACK, S], F32)
         c = [sb("c%d" % ci, [P, PACK, w], F32) for ci, (c0, w) in enumerate(CHUNKS)]
         z = [sb("z%d" % ci, [P, PACK * w], BF16) for ci, (c0, w) in enumerate(CHUNKS)]
 
@@ -144,33 +146,34 @@ def tile_picked_twkeyflowbkmax_none_po_kernel(tc, x_words, x_scales, w1_words, w
             return w, slice(c0, c0 + w), slice(c0 // 16, (c0 + w) // 16)
 
         def differences(ci, t):
-            w, cols, lcols = span(ci)
-            y1 = pool.tile([P, w], F32, name="y1_%d_%d" % (ci, t), tag="y1_%d" % t, align_bytes=64)
-            y2 = pool.tile([P, w], F32, name="y2_%d_%d" % (ci, t), tag="y2_%d" % t, align_bytes=64)
-            nc.scalar.activation(y1[:], y[t][:].indirect(n1_sb[:, lcols]), COPY)
-            nc.scalar.activation(y2[:], y[t][:].indirect(n2_sb[:, lcols]), COPY)
-            eng = nc.gpsimd if [ci, t] in SUBS_ON_GPSIMD else nc.vector
-            eng.tensor_tensor(ab[:, 2 * t, cols], y1[:], y[t][:, cols], SUB)
-            eng.tensor_tensor(ab[:, 2 * t + 1, cols], y2[:], y[t][:, cols], SUB)
+            c0, w = HALVES[ci]
+            cols = slice(c0, c0 + w)
+            lcols = slice(c0 // 16, (c0 + w) // 16)
+            y12 = pool.tile([P, 2, w], F32, name="y12_%d_%d" % (ci, t), tag=("y12_%d" if ci == 0 else "d3_0_%d") % t, align_bytes=64)
+            nc.scalar.activation(y12[:, 0, :], y[t][:].indirect(n1_sb[:, lcols]), COPY)
+            nc.scalar.activation(y12[:, 1, :], y[t][:].indirect(n2_sb[:, lcols]), COPY)
+            nc.vector.tensor_tensor(ab[:, 2 * t : 2 * t + 2, cols], y12[:], y[t][:, cols].unsqueeze(1).to_broadcast([P, 2, w]), SUB)
 
-        def first_term(ci, t):
-            w, cols, lcols = span(ci)
-            nc.vector.scalar_tensor_tensor(e[ci][:, t, :], ab[:, 2 * t, cols], 2.0, dh[t][:, cols], MULT, MULT)
+        def first_term(half, t):
+            cols = slice(half[0], half[0] + half[1])
+            nc.vector.scalar_tensor_tensor(e[:, t, cols], ab[:, 2 * t, cols], 2.0, dh[t][:, cols], MULT, MULT)
 
         def second_term(ci, t):
             w, cols, lcols = span(ci)
             if [ci, t] in D3_ON_VECTOR:
                 nc.vector.tensor_tensor(c[ci][:, t, :], dh[t][:].indirect(n3_sb[:, lcols]), ab[:, 2 * t + 1, cols], MULT)
             else:
-                d3 = sb("d3_%d_%d" % (ci, t), [P, w], F32)
-                nc.scalar.activation(d3[:], dh[t][:].indirect(n3_sb[:, lcols]), COPY)
-                nc.vector.tensor_tensor(c[ci][:, t, :], d3[:], ab[:, 2 * t + 1, cols], MULT)
+                if ci < 2:
+                    d3[t] = pool.tile([P, S // 2], F32, name="d3_%d_%d" % (ci, t), tag="d3_0_%d" % t, align_bytes=64)
+                part = d3[t][:, cols.start % (S // 2) : cols.start % (S // 2) + w]
+                nc.scalar.activation(part, dh[t][:].indirect(n3_sb[:, lcols]), COPY)
+                nc.vector.tensor_tensor(c[ci][:, t, :], part, ab[:, 2 * t + 1, cols], MULT)
 
         def sum_terms(ci):
             nc.vector.tensor_tensor(
-                z[ci][:].rearrange("p (g i t) -> p g t i", i=4, t=PACK),
-                e[ci][:].rearrange("p t (g i) -> p g t i", i=4),
-                c[ci][:].rearrange("p t (g i) -> p g t i", i=4),
+                z[ci][:].rearrange("p (g i t) -> p g t i", i=2, t=PACK),
+                e[:, :, span(ci)[1]].rearrange("p t (g i) -> p g t i", i=2),
+                c[ci][:].rearrange("p t (g i) -> p g t i", i=2),
                 ADD,
             )
 
@@ -183,25 +186,38 @@ def tile_picked_twkeyflowbkmax_none_po_kernel(tc, x_words, x_scales, w1_words, w
                 mx(h_ps[t][:, cols], w2w_d, w2s_d, t, zw[:], zs[:])
 
         for t in range(PACK):
-            if t in DCOPY_ON_SCALAR:
-                nc.scalar.activation(dh[t][:], d_ps[t][:], COPY, scale=gn32[:, t : t + 1])
-            else:
+            if t not in DCOPY_ON_SCALAR:
                 nc.vector.tensor_scalar(dh[t][:], d_ps[t][:], gn32[:, t : t + 1], None, MULT)
         for t in range(PACK):
             nc.scalar.copy(y[t][:], y_ps[t][:])
+            if t == PACK - 1:
+                for u in range(PACK - 1):
+                    first_term(HALVES[0], u)
             differences(0, t)
-            first_term(0, t)
+            h_ps.append(psum.tile([P, S], F32, name="h_ps%d" % t, tag="bank%d" % t))
+        for t in DCOPY_ON_SCALAR:
+            nc.scalar.activation(dh[t][:], d_ps[t][:], COPY, scale=gn32[:, t : t + 1])
+        deal(nc.vector, w2w_d, w2w)
+        deal_words(nc.vector, w2s_d, w2s)
+        first_term(HALVES[0], PACK - 1)
         for t in range(PACK):
             second_term(0, t)
-            h_ps.append(psum.tile([P, S], F32, name="h_ps%d" % t, tag="bank%d" % t))
-        for ci in range(1, len(CHUNKS)):
-            sum_terms(ci - 1)
-            for t in range(PACK):
-                differences(ci, t)
-                if t == 0:
-                    last_product(ci - 1)
-                first_term(ci, t)
-                second_term(ci, t)
+        for t in range(PACK):
+            differences(1, t)
+            if t == 0:
+                sum_terms(0)
+            if t == 1:
+                last_product(0)
+        for t in range(PACK):
+            first_term(HALVES[1], t)
+        for t in range(PACK):
+            second_term(1, t)
+        for t in range(PACK):
+            second_term(2, t)
+            if t == 0:
+                sum_terms(1)
+            if t == 1:
+                last_product(1)
         last = len(CHUNKS) - 1
         sum_terms(last)
         early = slice(0, CHUNKS[last][0])

@@ -22,9 +22,10 @@ P = 128
 PACK = 4
 CHUNKS = [[0,256],[256,128],[384,128]]
 HALVES = [[0, 256], [256, 256]]
-DCOPY_ON_SCALAR = [3]
+DCOPY_ON_SCALAR = []
 D3_ON_VECTOR = []
-SUBS_ON_GPSIMD = []
+SUBS_ON_GPSIMD = [0,1,2,3]
+YCOPY_ON_VECTOR = [3]
 
 
 def tile_picked_twkeyflowbkmax_none_po_kernel(tc, x_words, x_scales, w1_words, w1_scales, d_words, d_scales, gn, w2_words, w2_scales, offs, k1, two, n1, n2, n3, n4, n5, out_0, out_1, out_2):
@@ -85,8 +86,10 @@ def tile_picked_twkeyflowbkmax_none_po_kernel(tc, x_words, x_scales, w1_words, w
         n5_sb = load_list("n5_sb", n5)
 
         gn32 = sb("gn32", [P, PACK], F32)
-        nc.scalar.activation(gn32[:], gn_sb[:], COPY, scale=0.03125)
+        nc.gpsimd.tensor_scalar(gn32[:], gn_sb[:], 0.03125, 0.0, MULT, ADD)
 
+        gn16 = sb("gn16", [P, PACK], F32)
+        nc.gpsimd.tensor_scalar(gn16[:], gn_sb[:], 0.0625, 0.0, MULT, ADD)
         xs_offs = sb("xs_offs", [P, S], U8)
         xw_offs = sb("xw_offs", [P, S], I32)
         xs_two = sb("xs_two", [P, S], U8)
@@ -95,8 +98,6 @@ def tile_picked_twkeyflowbkmax_none_po_kernel(tc, x_words, x_scales, w1_words, w
         dw_k1 = sb("dw_k1", [P, H], I32)
         w1s_d = sb("w1s_d", [P, H], U8)
         w1w_d = sb("w1w_d", [P, H], I32)
-        w2s_d = sb("w2s_d", [P, N], U8)
-        w2w_d = sb("w2w_d", [P, N], I32)
         ds_d = sb("ds_d", [P, H], U8)
         dw_d = sb("dw_d", [P, H], I32)
 
@@ -124,39 +125,47 @@ def tile_picked_twkeyflowbkmax_none_po_kernel(tc, x_words, x_scales, w1_words, w
         deal(nc.vector, dw_d, dw_k1)
         w2w = pool.tile([P, N], I32, name="w2w", tag="ds_k1", align_bytes=64)
         nc.sync.dma_start(w2w[:], words_of(w2_words))
-        w2s = pool.tile([P, N], U8, name="w2s", tag="dw_k1", align_bytes=64)
+        w2s = pool.tile([P, N], U8, name="w2s", tag="xw", align_bytes=64)
         load_plane_everywhere(w2s, w2_scales)
 
         d_ps = [psum.tile([P, S], F32, name="d_ps%d" % t, tag="bank%d" % (PACK + t)) for t in range(PACK)]
         for t in range(PACK):
             mx(d_ps[t][:], dw_d, ds_p, t, xw_two[:], xs_two[:])
 
-        y = [sb("y%d" % t, [P, S], F32) for t in range(PACK)]
+        y = [sb("y%d" % t, [P, S], F32) for t in range(PACK - 1)]
+        y.append(pool.tile([P, S], F32, name="y3", tag="dw", align_bytes=64))
         dh = [sb("dh%d" % t, [P, S], F32) for t in range(PACK)]
         h = [sb("h%d" % t, [P, S], F32) for t in range(PACK)]
-        ab = pool.tile([P, 2 * PACK, S], F32, name="ab", tag="dw", align_bytes=64)
+        ab = pool.tile([P, 2 * PACK, S], F32, name="ab", tag="dw_k1", align_bytes=64)
         h_ps = []
         d3 = [None] * PACK
         e = sb("e", [P, PACK, S], F32)
-        c = [sb("c%d" % ci, [P, PACK, w], F32) for ci, (c0, w) in enumerate(CHUNKS)]
+        c = [None] + [sb("c%d" % ci, [P, PACK, CHUNKS[ci][1]], F32) for ci in (1, 2)]
         z = [sb("z%d" % ci, [P, PACK * w], BF16) for ci, (c0, w) in enumerate(CHUNKS)]
 
         def span(ci):
             c0, w = CHUNKS[ci]
             return w, slice(c0, c0 + w), slice(c0 // 16, (c0 + w) // 16)
 
+        def second_slot(t):
+            return "d3_0_%d" % t
+
         def differences(ci, t):
             c0, w = HALVES[ci]
             cols = slice(c0, c0 + w)
             lcols = slice(c0 // 16, (c0 + w) // 16)
-            y12 = pool.tile([P, 2, w], F32, name="y12_%d_%d" % (ci, t), tag=("y12_%d" if ci == 0 else "d3_0_%d") % t, align_bytes=64)
+            y12 = pool.tile([P, 2, w], F32, name="y12_%d_%d" % (ci, t), tag=("y12_%d" % t if ci == 0 else second_slot(t)), align_bytes=64)
             nc.scalar.activation(y12[:, 0, :], y[t][:].indirect(n1_sb[:, lcols]), COPY)
             nc.scalar.activation(y12[:, 1, :], y[t][:].indirect(n2_sb[:, lcols]), COPY)
-            nc.vector.tensor_tensor(ab[:, 2 * t : 2 * t + 2, cols], y12[:], y[t][:, cols].unsqueeze(1).to_broadcast([P, 2, w]), SUB)
+            eng = nc.gpsimd if ci == 0 and t in SUBS_ON_GPSIMD else nc.vector
+            eng.tensor_tensor(ab[:, 2 * t : 2 * t + 2, cols], y12[:], y[t][:, cols].unsqueeze(1).to_broadcast([P, 2, w]), SUB)
 
         def first_term(half, t):
             cols = slice(half[0], half[0] + half[1])
-            nc.vector.scalar_tensor_tensor(e[:, t, cols], ab[:, 2 * t, cols], 2.0, dh[t][:, cols], MULT, MULT)
+            if half[0] == 0:
+                nc.vector.scalar_tensor_tensor(e[:, t, cols], d_ps[t][:, cols], gn16[:, t : t + 1], ab[:, 2 * t, cols], MULT, MULT)
+            else:
+                nc.vector.scalar_tensor_tensor(e[:, t, cols], ab[:, 2 * t, cols], 2.0, dh[t][:, cols], MULT, MULT)
 
         def second_term(ci, t):
             w, cols, lcols = span(ci)
@@ -164,7 +173,7 @@ def tile_picked_twkeyflowbkmax_none_po_kernel(tc, x_words, x_scales, w1_words, w
                 nc.vector.tensor_tensor(c[ci][:, t, :], dh[t][:].indirect(n3_sb[:, lcols]), ab[:, 2 * t + 1, cols], MULT)
             else:
                 if ci < 2:
-                    d3[t] = pool.tile([P, S // 2], F32, name="d3_%d_%d" % (ci, t), tag="d3_0_%d" % t, align_bytes=64)
+                    d3[t] = pool.tile([P, S // 2], F32, name="d3_%d_%d" % (ci, t), tag=("d3_0_%d" % t if ci == 0 else second_slot(t)), align_bytes=64)
                 part = d3[t][:, cols.start % (S // 2) : cols.start % (S // 2) + w]
                 nc.scalar.activation(part, dh[t][:].indirect(n3_sb[:, lcols]), COPY)
                 nc.vector.tensor_tensor(c[ci][:, t, :], part, ab[:, 2 * t + 1, cols], MULT)
@@ -189,7 +198,10 @@ def tile_picked_twkeyflowbkmax_none_po_kernel(tc, x_words, x_scales, w1_words, w
             if t not in DCOPY_ON_SCALAR:
                 nc.vector.tensor_scalar(dh[t][:], d_ps[t][:], gn32[:, t : t + 1], None, MULT)
         for t in range(PACK):
-            nc.scalar.copy(y[t][:], y_ps[t][:])
+            if t in YCOPY_ON_VECTOR:
+                nc.vector.tensor_copy(y[t][:], y_ps[t][:])
+            else:
+                nc.scalar.copy(y[t][:], y_ps[t][:])
             if t == PACK - 1:
                 for u in range(PACK - 1):
                     first_term(HALVES[0], u)
@@ -197,16 +209,18 @@ def tile_picked_twkeyflowbkmax_none_po_kernel(tc, x_words, x_scales, w1_words, w
             h_ps.append(psum.tile([P, S], F32, name="h_ps%d" % t, tag="bank%d" % t))
         for t in DCOPY_ON_SCALAR:
             nc.scalar.activation(dh[t][:], d_ps[t][:], COPY, scale=gn32[:, t : t + 1])
+        w2w_d = sb("w2w_d", [P, N], I32)
+        w2s_d = sb("w2s_d", [P, N], U8)
         deal(nc.vector, w2w_d, w2w)
         deal_words(nc.vector, w2s_d, w2s)
         first_term(HALVES[0], PACK - 1)
+        c[0] = pool.tile([P, PACK, CHUNKS[0][1]], F32, name="c0", tag="y12_3", align_bytes=64)
         for t in range(PACK):
             second_term(0, t)
+        sum_terms(0)
         for t in range(PACK):
             differences(1, t)
             if t == 0:
-                sum_terms(0)
-            if t == 1:
                 last_product(0)
         for t in range(PACK):
             first_term(HALVES[1], t)
@@ -240,17 +254,23 @@ def tile_picked_twkeyflowbkmax_none_po_kernel(tc, x_words, x_scales, w1_words, w
         def put_back(t):
             nc.scalar.activation(h[t][:].indirect(n4_sb[:]), ra[t][:], COPY)
             nc.sync.dma_start(out_rows[t], h[t][:])
-            nc.vector.tensor_copy(ob[:, :, t], h[t][:])
+            if t < PACK - 1:
+                nc.vector.tensor_copy(ob[:, :, t], h[t][:])
+            else:
+                nc.vector.tensor_copy(ob[:, 0:256, t], h[t][:, 0:256])
+                nc.vector.tensor_copy(ob[:, 256:512, t], h[t][:, 256:512])
 
         look_up(0)
         for t in range(PACK):
             if t + 1 < PACK:
                 look_up(t + 1)
             put_back(t)
-        ow = sb("ow", [P, S], I32)
         osc = sb("osc", [P, S], U8)
-        nc.vector.quantize_mx(ow[:].bitcast(FP8X4), osc[:], ob[:].rearrange("p n t -> p (n t)"))
-        nc.sync.dma_start(words_of(out_1), ow[:])
+        for i in range(2):
+            cols = slice(256 * i, 256 * (i + 1))
+            ow = sb("ow%d" % i, [P, 256], I32)
+            nc.vector.quantize_mx(ow[:].bitcast(FP8X4), osc[:, cols], ob[:, cols, :].rearrange("p n t -> p (n t)"))
+            nc.sync.dma_start(words_of(out_1)[:, cols], ow[:])
         for q in range(4):
             eng = nc.scalar if q % 2 == 0 else nc.sync
             eng.dma_start(out_2[0][4 * q : 4 * q + 4, :].bitcast(I32), osc[32 * q : 32 * q + 4, :].bitcast(I32))

from contextlib import ExitStack

import concourse.mybir as mybir

K, T, S, N, H, G, W = 512, 2048, 512, 512, 512, 2048, 384
FLOPS = 2 * K * H * S * 2 + 2 * H * N * S

F32 = mybir.dt.float32
BF16 = mybir.dt.bfloat16
I32 = mybir.dt.int32
U32 = mybir.dt.uint32
U16 = mybir.dt.uint16
U8 = mybir.dt.uint8
FP8X4 = mybir.dt.float8_e4m3fn_x4
MULT = mybir.AluOpType.mult
ADD = mybir.AluOpType.add
SUB = mybir.AluOpType.subtract
MAX = mybir.AluOpType.max
COPY = mybir.ActivationFunctionType.Copy

P = 128
PACK = 4
CHUNKS = [[0,256],[256,128],[384,128]]
HALVES = [[0, 256], [256, 256]]
DCOPY_ON_SCALAR = []
D3_ON_VECTOR = []
SUBS_ON_GPSIMD = [0,1,2,3]
YCOPY_ON_VECTOR = [3]


def tile_picked_twkeyflowbkmax_none_po_kernel(tc, x_words, x_scales, w1_words, w1_scales, d_words, d_scales, gn, w2_words, w2_scales, offs, k1, two, n1, n2, n3, n4, n5, out_0, out_1, out_2):
    nc = tc.nc
    with ExitStack() as ctx:
        pool = ctx.enter_context(tc.tile_pool(name="pool", bufs=1))
        psum = ctx.enter_context(tc.psum_pool(name="psum", bufs=1))

        def sb(name, shape, dtype):
            return pool.tile(shape, dtype, name=name, align_bytes=64)

        def load_list(name, src):
            t = sb(name, list(src.shape), U16)
            nc.sync.dma_start(t[:], src)
            return t

        def words_of(src):
            return src[0].rearrange("p n r -> p (n r)").bitcast(I32)

        def load_plane(eng, dst, src, k=0):
            for q in range(4):
                eng.dma_start(dst[32 * q + k : 32 * q + k + 4, :].bitcast(I32), src[0][4 * q : 4 * q + 4, :].bitcast(I32))

        def load_plane_everywhere(dst, src):
            for q in range(4):
                rows = src[0][4 * q : 4 * q + 4, :].bitcast(I32)
                nc.sync.dma_start(dst[32 * q : 32 * q + 32, :].bitcast(I32), rows.unsqueeze(0).to_broadcast([8, 4, rows.shape[1]]))

        def deal(eng, dst, src):
            eng.tensor_copy(dst[:].rearrange("p (t m) -> p m t", t=PACK), src[:].rearrange("p (m t) -> p m t", t=PACK))

        def deal_words(eng, dst, src):
            eng.tensor_copy(dst[:].rearrange("p (t m) -> p t m", t=PACK), src[:].rearrange("p (m t) -> p t m", t=PACK))

        xs = sb("xs", [P, T], U8)
        w1s = sb("w1s", [P, H], U8)
        ds = sb("ds", [P, G], U8)
        nc.vector.memset(ds[:].bitcast(I32), 0)

        xw = sb("xw", [P, T], I32)
        dw = sb("dw", [P, G], I32)
        w1w = sb("w1w", [P, H], I32)
        gn_sb = sb("gn_sb", [P, PACK], F32)
        load_plane_everywhere(xs, x_scales)
        offs_sb = load_list("offs_sb", offs)
        k1_sb = load_list("k1_sb", k1)
        nc.sync.dma_start(ds[0:P:8, :].bitcast(I32), d_scales[0].bitcast(I32))
        nc.sync.dma_start(xw[:], words_of(x_words))
        nc.sync.dma_start(w1w[:], words_of(w1_words))
        load_plane_everywhere(w1s, w1_scales)
        n1_sb = load_list("n1_sb", n1)
        n2_sb = load_list("n2_sb", n2)
        two_sb = load_list("two_sb", two)
        nc.sync.dma_start(dw[:], words_of(d_words))
        nc.sync.dma_start(gn_sb[:], gn.rearrange("(p t) o -> p (t o)", t=PACK))
        n3_sb = load_list("n3_sb", n3)
        n4_sb = load_list("n4_sb", n4)
        n5_sb = load_list("n5_sb", n5)

        gn32 = sb("gn32", [P, PACK], F32)
        nc.gpsimd.tensor_scalar(gn32[:], gn_sb[:], 0.03125, 0.0, MULT, ADD)

        gn16 = sb("gn16", [P, PACK], F32)
        nc.gpsimd.tensor_scalar(gn16[:], gn_sb[:], 0.0625, 0.0, MULT, ADD)
        xs_offs = sb("xs_offs", [P, S], U8)
        xw_offs = sb("xw_offs", [P, S], I32)
        xs_two = sb("xs_two", [P, S], U8)
        xw_two = sb("xw_two", [P, S], I32)
        ds_k1 = sb("ds_k1", [P, H], U8)
        dw_k1 = sb("dw_k1", [P, H], I32)
        w1s_d = sb("w1s_d", [P, H], U8)
        w1w_d = sb("w1w_d", [P, H], I32)
        ds_d = sb("ds_d", [P, H], U8)
        dw_d = sb("dw_d", [P, H], I32)

        nc.vector.tensor_copy(xs_offs[:], xs[:].indirect(offs_sb[:]))
        nc.vector.tensor_copy(ds_k1[:], ds[:].indirect(k1_sb[:]))
        deal_words(nc.vector, ds_d, ds_k1)
        nc.vector.tensor_copy(xw_offs[:].bitcast(U32), xw[:].bitcast(U32).indirect(offs_sb[:]))
        deal(nc.vector, w1w_d, w1w)
        deal_words(nc.vector, w1s_d, w1s)
        ds_p = ds_d
        for j in range(1, 4):
            nc.sync.dma_start(ds_p[j:P:32, :].bitcast(I32), ds_d[8 * j : P : 32, :].bitcast(I32))

        def mx(out, w, ws, t, x, xsc):
            cols = slice(P * t, P * (t + 1))
            nc.tensor.matmul_mx(out, w[:, cols].bitcast(FP8X4), ws[:, cols], x.bitcast(FP8X4), xsc, start=True, stop=True)

        y_ps = [psum.tile([P, S], F32, name="y_ps%d" % t, tag="bank%d" % t) for t in range(PACK)]
        for t in range(PACK):
            mx(y_ps[t][:], w1w_d, w1s_d, t, xw_offs[:], xs_offs[:])

        nc.vector.tensor_copy(xs_two[:], xs[:].indirect(two_sb[:]))
        nc.vector.tensor_copy(xw_two[:].bitcast(U32), xw[:].bitcast(U32).indirect(two_sb[:]))
        nc.vector.tensor_copy(dw_k1[:].bitcast(U32), dw[:].bitcast(U32).indirect(k1_sb[:]))
        deal(nc.vector, dw_d, dw_k1)
        w2w = pool.tile([P, N], I32, name="w2w", tag="ds_k1", align_bytes=64)
        nc.sync.dma_start(w2w[:], words_of(w2_words))
        w2s = pool.tile([P, N], U8, name="w2s", tag="xw", align_bytes=64)
        load_plane_everywhere(w2s, w2_scales)

        d_ps = [psum.tile([P, S], F32, name="d_ps%d" % t, tag="bank%d" % (PACK + t)) for t in range(PACK)]
        for t in range(PACK):
            mx(d_ps[t][:], dw_d, ds_p, t, xw_two[:], xs_two[:])

        y = [sb("y%d" % t, [P, S], F32) for t in range(PACK - 1)]
        y.append(pool.tile([P, S], F32, name="y3", tag="dw", align_bytes=64))
        dh = [sb("dh%d" % t, [P, S], F32) for t in range(PACK)]
        h = [sb("h%d" % t, [P, S], F32) for t in range(PACK)]
        ab = pool.tile([P, 2 * PACK, S], F32, name="ab", tag="dw_k1", align_bytes=64)
        h_ps = []
        d3 = [None] * PACK
        e = sb("e", [P, PACK, S], F32)
        c = [None] + [sb("c%d" % ci, [P, PACK, CHUNKS[ci][1]], F32) for ci in (1, 2)]
        z = [sb("z%d" % ci, [P, PACK * w], BF16) for ci, (c0, w) in enumerate(CHUNKS)]

        def span(ci):
            c0, w = CHUNKS[ci]
            return w, slice(c0, c0 + w), slice(c0 // 16, (c0 + w) // 16)

        def second_slot(t):
            return "d3_0_%d" % t

        def differences(ci, t):
            c0, w = HALVES[ci]
            cols = slice(c0, c0 + w)
            lcols = slice(c0 // 16, (c0 + w) // 16)
            y12 = pool.tile([P, 2, w], F32, name="y12_%d_%d" % (ci, t), tag=("y12_%d" % t if ci == 0 else second_slot(t)), align_bytes=64)
            nc.scalar.activation(y12[:, 0, :], y[t][:].indirect(n1_sb[:, lcols]), COPY)
            nc.scalar.activation(y12[:, 1, :], y[t][:].indirect(n2_sb[:, lcols]), COPY)
            eng = nc.gpsimd if ci == 0 and t in SUBS_ON_GPSIMD else nc.vector
            eng.tensor_tensor(ab[:, 2 * t : 2 * t + 2, cols], y12[:], y[t][:, cols].unsqueeze(1).to_broadcast([P, 2, w]), SUB)

        def first_term(half, t):
            cols = slice(half[0], half[0] + half[1])
            if half[0] == 0:
                nc.vector.scalar_tensor_tensor(e[:, t, cols], d_ps[t][:, cols], gn16[:, t : t + 1], ab[:, 2 * t, cols], MULT, MULT)
            else:
                nc.vector.scalar_tensor_tensor(e[:, t, cols], ab[:, 2 * t, cols], 2.0, dh[t][:, cols], MULT, MULT)

        def second_term(ci, t):
            w, cols, lcols = span(ci)
            if [ci, t] in D3_ON_VECTOR:
                nc.vector.tensor_tensor(c[ci][:, t, :], dh[t][:].indirect(n3_sb[:, lcols]), ab[:, 2 * t + 1, cols], MULT)
            else:
                if ci < 2:
                    d3[t] = pool.tile([P, S // 2], F32, name="d3_%d_%d" % (ci, t), tag=("d3_0_%d" % t if ci == 0 else second_slot(t)), align_bytes=64)
                part = d3[t][:, cols.start % (S // 2) : cols.start % (S // 2) + w]
                nc.scalar.activation(part, dh[t][:].indirect(n3_sb[:, lcols]), COPY)
                nc.vector.tensor_tensor(c[ci][:, t, :], part, ab[:, 2 * t + 1, cols], MULT)

        def sum_terms(ci):
            nc.vector.tensor_tensor(
                z[ci][:].rearrange("p (g i t) -> p g t i", i=2, t=PACK),
                e[:, :, span(ci)[1]].rearrange("p t (g i) -> p g t i", i=2),
                c[ci][:].rearrange("p t (g i) -> p g t i", i=2),
                ADD,
            )

        def last_product(ci):
            w, cols, lcols = span(ci)
            zw = sb("zw%d" % ci, [P, w], I32)
            zs = sb("zs%d" % ci, [P, w], U8)
            nc.vector.quantize_mx(zw[:].bitcast(FP8X4), zs[:], z[ci][:])
            for t in range(PACK):
                mx(h_ps[t][:, cols], w2w_d, w2s_d, t, zw[:], zs[:])

        for t in range(PACK):
            if t not in DCOPY_ON_SCALAR:
                nc.vector.tensor_scalar(dh[t][:], d_ps[t][:], gn32[:, t : t + 1], None, MULT)
        for t in range(PACK):
            if t in YCOPY_ON_VECTOR:
                nc.vector.tensor_copy(y[t][:], y_ps[t][:])
            else:
                nc.scalar.copy(y[t][:], y_ps[t][:])
            if t == PACK - 1:
                for u in range(PACK - 1):
                    first_term(HALVES[0], u)
            differences(0, t)
            h_ps.append(psum.tile([P, S], F32, name="h_ps%d" % t, tag="bank%d" % t))
        for t in DCOPY_ON_SCALAR:
            nc.scalar.activation(dh[t][:], d_ps[t][:], COPY, scale=gn32[:, t : t + 1])
        w2w_d = sb("w2w_d", [P, N], I32)
        w2s_d = sb("w2s_d", [P, N], U8)
        deal(nc.vector, w2w_d, w2w)
        deal_words(nc.vector, w2s_d, w2s)
        first_term(HALVES[0], PACK - 1)
        c[0] = pool.tile([P, PACK, CHUNKS[0][1]], F32, name="c0", tag="y12_3", align_bytes=64)
        for t in range(PACK):
            second_term(0, t)
        sum_terms(0)
        for t in range(PACK):
            differences(1, t)
            if t == 0:
                last_product(0)
        for t in range(PACK):
            first_term(HALVES[1], t)
        for t in range(PACK):
            second_term(1, t)
        for t in range(PACK):
            second_term(2, t)
            if t == 0:
                sum_terms(1)
            if t == 1:
                last_product(1)
        last = len(CHUNKS) - 1
        sum_terms(last)
        early = slice(0, CHUNKS[last][0])
        nc.scalar.copy(h[0][:, early], h_ps[0][:, early])
        last_product(last)
        nc.scalar.copy(h[0][:, span(last)[1]], h_ps[0][:, span(last)[1]])

        ob = sb("ob", [P, S, PACK], BF16)
        out_rows = out_0.rearrange("(p t) n -> t p n", t=PACK)
        old = [sb("old%d" % t, [P, W], F32) for t in range(PACK)]
        pa = [sb("pa%d" % t, [P, W], F32) for t in range(PACK)]
        ra = [sb("ra%d" % t, [P, W], F32) for t in range(PACK)]
        def look_up(t):
            if t > 0:
                nc.vector.tensor_copy(h[t][:], h_ps[t][:])
            nc.scalar.activation(old[t][:], h[t][:].indirect(n4_sb[:]), COPY)
            nc.vector.tensor_copy(pa[t][:], h[t][:].indirect(n5_sb[:]))
            nc.vector.scalar_tensor_tensor(ra[t][:], old[t][:], 0.5, pa[t][:], MULT, MAX)

        def put_back(t):
            nc.scalar.activation(h[t][:].indirect(n4_sb[:]), ra[t][:], COPY)
            nc.sync.dma_start(out_rows[t], h[t][:])
            if t < PACK - 1:
                nc.vector.tensor_copy(ob[:, :, t], h[t][:])
            else:
                nc.vector.tensor_copy(ob[:, 0:256, t], h[t][:, 0:256])
                nc.vector.tensor_copy(ob[:, 256:512, t], h[t][:, 256:512])

        look_up(0)
        for t in range(PACK):
            if t + 1 < PACK:
                look_up(t + 1)
            put_back(t)
        osc = sb("osc", [P, S], U8)
        for i in range(2):
            cols = slice(256 * i, 256 * (i + 1))
            ow = sb("ow%d" % i, [P, 256], I32)
            nc.vector.quantize_mx(ow[:].bitcast(FP8X4), osc[:, cols], ob[:, cols, :].rearrange("p n t -> p (n t)"))
            nc.sync.dma_start(words_of(out_1)[:, cols], ow[:])
        for q in range(4):
            eng = nc.scalar if q % 2 == 0 else nc.sync
            eng.dma_start(out_2[0][4 * q : 4 * q + 4, :].bitcast(I32), osc[32 * q : 32 * q + 4, :].bitcast(I32))
